import numpy as np
import ml_dtypes


def mxq(x, axis, fmt="e4m3"):
    dtype, down = {"e4m3": (ml_dtypes.float8_e4m3fn, 7), "e5m2": (ml_dtypes.float8_e5m2, 14)}[fmt]
    v = np.moveaxis(np.asarray(x, np.float32).astype(ml_dtypes.bfloat16).astype(np.float64), axis, -1)
    blocks = v.reshape(v.shape[:-1] + (-1, 32))
    amax = np.abs(blocks).max(-1, keepdims=True)
    byte = np.maximum(np.where(amax > 0, np.frexp(amax)[1] - 1 + 127, 0) - down, 1)
    scale = np.exp2(byte - 127.0)
    codes = (blocks / scale).astype(np.float32).astype(dtype).astype(np.float64)
    return np.moveaxis((codes * scale).reshape(v.shape), -1, axis)


WIDE = False


def mx_kscale(k):
    if not WIDE:
        return np.ones(k)
    levels = np.array([30, -30])
    if k % 512:
        return np.exp2(np.random.permutation(np.resize(levels, k // 32))).repeat(32)
    a = np.empty((k // 512, 16))
    for p in range(k // 512):
        a[p, :8] = np.random.permutation(np.resize(levels, 8))
        for g in range(8):
            far = levels[np.abs(levels - a[p, g]) >= 10]
            a[p, g + 8] = far[np.random.randint(len(far))]
    return np.exp2(a.ravel()).repeat(32)


def f64(x):
    return np.asarray(x).astype(np.float64)


def striped(idx):
    return np.tile(np.asarray(idx).reshape(-1, 16).T, (8, 1)).astype(np.uint16)


def unstriped(offs):
    return offs[:16].T.reshape(-1).astype(np.int64)


E2M1 = np.array([0.0, 0.5, 1.0, 1.5, 2.0, 3.0, 4.0, 6.0, -0.0, -0.5, -1.0, -1.5, -2.0, -3.0, -4.0, -6.0])


def pack_weight(w, fmt):
    k, n = w.shape
    w = f64(np.asarray(w, np.float32).astype(ml_dtypes.bfloat16)).reshape(k // 32, 32, n)
    amax = np.abs(w).max(1)
    if fmt in ("e4m3", "e5m2"):
        byte = np.frexp(amax)[1] - 1 + 127 - (7 if fmt == "e4m3" else 14)
    else:
        mant, ex = np.frexp(amax / 6.0)
        byte = np.where(mant > 0.5, ex, ex - 1) + 127
    byte = np.clip(np.where(amax > 0, byte, 1), 1, 254)
    scaled = (w * np.exp2(127.0 - byte)[:, None, :]).reshape(k, n).astype(np.float32)
    by_word = np.ascontiguousarray(scaled.reshape(k // 512, 128, 4, n).transpose(0, 1, 3, 2))
    if fmt in ("e4m3", "e5m2"):
        words = by_word.astype(ml_dtypes.float8_e4m3fn if fmt == "e4m3" else ml_dtypes.float8_e5m2).view(np.uint8)
    else:
        c = by_word.astype(ml_dtypes.float4_e2m1fn).view(np.uint8) & 0xF
        words = (c[..., 0::2] | (c[..., 1::2] << 4)).reshape(k // 512, 128, 2 * n)
    return np.ascontiguousarray(words), np.ascontiguousarray(byte.astype(np.uint8).reshape(k // 512, 16, n))


def unpack_weight(words, scales, fmt):
    g, _, n = scales.shape
    words = np.ascontiguousarray(words).reshape(g, 128, n, -1)
    if fmt in ("e4m3", "e5m2"):
        vals = words.view(ml_dtypes.float8_e4m3fn if fmt == "e4m3" else ml_dtypes.float8_e5m2).astype(np.float64)
    else:
        nib = np.empty((g, 128, n, 4), np.uint8)
        nib[..., 0::2] = words & 0xF
        nib[..., 1::2] = words >> 4
        vals = E2M1[nib]
    vals = vals * np.repeat(np.exp2(scales.astype(np.float64) - 127.0), 8, axis=1)[..., None]
    return vals.transpose(0, 1, 3, 2).reshape(g * 512, n)


def e4m3fn_bytes(y):
    return np.clip(np.asarray(y, np.float64), -448.0, 448.0).astype(np.float32).astype(ml_dtypes.float8_e4m3fn).view(np.uint8)


def e4m3fn_values(b):
    return np.asarray(b, np.uint8).view(ml_dtypes.float8_e4m3fn).astype(np.float64)


K, T, J, R, V, D, U, E = 512, 2048, 256, 512, 1024, 1024, 256, 512


def setup_inputs():
    n = np.random.standard_normal
    idx = np.random.permutation(T)[:J]
    idx2 = np.random.permutation(T)[:J]
    idx3 = np.random.permutation(V)[:U]
    idx4 = np.random.permutation(D)[:U]
    idx5 = np.random.permutation(E)[:U]
    fk = mx_kscale(K)
    fr = mx_kscale(R)
    xtp = pack_weight(n((K, T)) / fk[:, None], "e5m2")
    wp = pack_weight(n((K, R)) * 1 / np.sqrt(K) * fk[:, None] * fr, "e2m1")
    w2p = pack_weight(n((K, R)) * 1 / np.sqrt(K) * fk[:, None] * fr, "e4m3")
    return {
        "xt_words": xtp[0],
        "xt_scales": xtp[1],
        "w_words": wp[0],
        "w_scales": wp[1],
        "w2_words": w2p[0],
        "w2_scales": w2p[1],
        "ca": e4m3fn_bytes(60.0 * n((R, V))),
        "cb": e4m3fn_bytes(60.0 * n((R, D))),
        "sa": (np.random.uniform(0.0002, 0.0006, (R, 1)) / fr[:, None]).astype(np.float32),
        "sb": (np.random.uniform(0.0002, 0.0006, (R, 1)) / fr[:, None]).astype(np.float32),
        "sz": (np.random.uniform(0.5, 1.6, (J, 1))).astype(np.float32),
        "offs": striped(idx),
        "offs2": striped(idx2),
        "offs3": striped(idx3),
        "offs4": striped(idx4),
        "offs5": striped(idx5),
    }


def reference(xt_words, xt_scales, w_words, w_scales, w2_words, w2_scales, ca, cb, sa, sb, sz, offs, offs2, offs3, offs4, offs5):
    idx = unstriped(offs)
    idx2 = unstriped(offs2)
    idx3 = unstriped(offs3)
    idx4 = unstriped(offs4)
    idx5 = unstriped(offs5)
    xtu = unpack_weight(xt_words, xt_scales, "e5m2")
    wu = unpack_weight(w_words, w_scales, "e2m1")
    w2u = unpack_weight(w2_words, w2_scales, "e4m3")
    xtidxg = xtu[:, idx]
    a = wu.T @ xtidxg
    xtidx2g = xtu[:, idx2]
    b = w2u.T @ xtidx2g
    ka = e4m3fn_values(ca)[:, idx3] * f64(sa)
    kb = e4m3fn_values(cb)[:, idx4] * f64(sb)
    aq = mxq(a, 0, "e4m3")
    kaq = mxq(ka, 0, "e4m3")
    bq = mxq(b, 0, "e4m3")
    kbq = mxq(kb, 0, "e4m3")
    p = aq.T @ kaq + bq.T @ kbq
    y = np.zeros((J, E))
    y[:, idx5] = p * f64(sz)
    return y

@@ -1,0 +1,178 @@
+from contextlib import ExitStack
+
+import concourse.mybir as mybir
+
+K, T, J, R, V, U, E = 512, 2048, 256, 512, 1024, 256, 512
+FLOPS = 2 * (2 * K * R * J) + 2 * (2 * R * J * U)
+
+F32 = mybir.dt.float32
+BF16 = mybir.dt.bfloat16
+I32 = mybir.dt.int32
+U32 = mybir.dt.uint32
+U16 = mybir.dt.uint16
+U8 = mybir.dt.uint8
+FP8 = mybir.dt.float8_e4m3fn
+E4M3X4 = mybir.dt.float8_e4m3fn_x4
+E5M2X4 = mybir.dt.float8_e5m2_x4
+E2M1X4 = mybir.dt.float4_e2m1fn_x4
+COPY = mybir.ActivationFunctionType.Copy
+MULT = mybir.AluOpType.mult
+
+P = 128
+PACK = 4
+HALF = 128
+
+
+def tile_list_scoredboth_kernel(tc, xt_words, xt_scales, w_words, w_scales, w2_words, w2_scales, ca, cb, sa, sb, sz,
+                                   offs, offs2, offs3, offs4, offs5, out):
+    nc = tc.nc
+    with ExitStack() as ctx:
+        pool = ctx.enter_context(tc.tile_pool(name="pool", bufs=1))
+        psum = ctx.enter_context(tc.psum_pool(name="psum", bufs=1))
+
+        def sbuf(name, shape, dtype):
+            return pool.tile(shape, dtype, name=name, align_bytes=64)
+
+        def load_list(name, src):
+            lst = sbuf(name, [P, 16], U16)
+            nc.sync.dma_start(lst[:], src)
+            return lst
+
+        def load_scale_rows(queue, plane, src, quads):
+            for q in quads:
+                queue.dma_start(plane[32 * q:32 * q + 4, :].bitcast(I32), src[0, 4 * q:4 * q + 4, :].bitcast(I32))
+
+        xs = sbuf("xs", [P, T], U8)
+        ws_raw = sbuf("ws_raw", [P, R], U8)
+        w2s_raw = sbuf("w2s_raw", [P, R], U8)
+        pages = [sbuf("page%d" % h, [P, E], F32) for h in range(2)]
+        nc.vector.memset(xs[:].bitcast(I32), 0)
+        nc.vector.memset(ws_raw[:].bitcast(I32), 0)
+        nc.vector.memset(w2s_raw[:].bitcast(I32), 0)
+        for h in range(2):
+            nc.vector.memset(pages[h][:], 0.0)
+
+        ca_rows = ca.rearrange("(p t) v -> t p v", t=PACK)
+        cb_rows = cb.rearrange("(p t) v -> t p v", t=PACK)
+        ca_t = [sbuf("ca%d" % t, [P, V], U8) for t in range(PACK)]
+        cb_t = [sbuf("cb%d" % t, [P, V], U8) for t in range(PACK)]
+        sa_t = sbuf("sa", [P, PACK], F32)
+        sb_t = sbuf("sb", [P, PACK], F32)
+        sz_t = sbuf("sz", [P, 2], F32)
+        xw = sbuf("xw", [P, T], U32)
+        w_raw = sbuf("w_raw", [P, 2 * R], U8)
+        w2_raw = sbuf("w2_raw", [P, R], U32)
+
+        l3 = load_list("l3", offs3)
+        nc.sync.dma_start(ca_t[0][:], ca_rows[0])
+        nc.sync.dma_start(ca_t[1][:], ca_rows[1])
+        nc.sync.dma_start(sa_t[:], sa.rearrange("(p t) o -> p (t o)", t=PACK))
+        nc.sync.dma_start(ca_t[2][:], ca_rows[2])
+        nc.sync.dma_start(ca_t[3][:], ca_rows[3])
+        nc.sync.dma_start(xw[:].bitcast(I32), xt_words[0].rearrange("p c r -> p (c r)").bitcast(I32))
+        l1 = load_list("l1", offs)
+        load_scale_rows(nc.sync, xs, xt_scales, range(4))
+        nc.sync.dma_start(w_raw[:].bitcast(I32), w_words[0].bitcast(I32))
+        l2 = load_list("l2", offs2)
+        nc.sync.dma_start(w2_raw[:].bitcast(I32), w2_words[0].rearrange("p c r -> p (c r)").bitcast(I32))
+        load_scale_rows(nc.sync, ws_raw, w_scales, range(4))
+        load_scale_rows(nc.sync, w2s_raw, w2_scales, range(4))
+        nc.sync.dma_start(cb_t[0][:], cb_rows[0])
+        l4 = load_list("l4", offs4)
+        nc.sync.dma_start(cb_t[1][:], cb_rows[1])
+        nc.sync.dma_start(sb_t[:], sb.rearrange("(p t) o -> p (t o)", t=PACK))
+        for t in range(2, PACK):
+            nc.sync.dma_start(cb_t[t][:], cb_rows[t])
+        l5 = load_list("l5", offs5)
+        with nc.allow_non_contiguous_dma(reason="one weight a slot"):
+            nc.sync.dma_start(sz_t[:], sz.rearrange("(h p) o -> p (h o)", h=2))
+
+        def quantize(name, grouped, width):
+            codes = sbuf(name + "_codes", [P, width], U32)
+            plane = sbuf(name + "_plane", [P, width], U8)
+            nc.vector.quantize_mx(out=codes[:].bitcast(E4M3X4), scales=plane[:], in_=grouped[:].rearrange("p u t -> p (u t)"))
+            return codes, plane
+
+        def interleave(copy, grouped, rows):
+            copy(grouped[:].rearrange("p (c i) t -> p c t i", i=4), rows[:].rearrange("p t (c i) -> p c t i", i=4))
+
+        ka_bytes = sbuf("ka_bytes", [P, PACK, U], U8)
+        ka_rows = sbuf("ka_rows", [P, PACK, U], BF16)
+        ka_grouped = sbuf("ka_grouped", [P, U, PACK], BF16)
+        for t in range(PACK):
+            nc.vector.tensor_copy(ka_bytes[:, t, :], ca_t[t][:].indirect(l3[:]))
+            nc.scalar.activation(ka_rows[:, t, :], ka_bytes[:, t, :].bitcast(FP8), COPY, scale=sa_t[:, t:t + 1])
+
+        w_dealt = sbuf("w_dealt", [P, 2 * R], U8)
+        ws_dealt = sbuf("ws_dealt", [P, R], U8)
+        w2_dealt = sbuf("w2_dealt", [P, R], U32)
+        w2s_dealt = sbuf("w2s_dealt", [P, R], U8)
+
+        def deal(copy, dst, src):
+            copy(dst.rearrange("p (t m) -> p t m", t=PACK), src.rearrange("p (m t) -> p t m", t=PACK))
+
+        def first_stage(name, lst, dealt_words, fmt, dealt_plane):
+            words = sbuf(name + "_xw", [P, J], U32)
+            plane = sbuf(name + "_xs", [P, J], U8)
+            nc.vector.tensor_copy(words[:], xw[:].indirect(lst[:]))
+            nc.vector.tensor_copy(plane[:], xs[:].indirect(lst[:]))
+            grouped = []
+            per = dealt_words.shape[1] // PACK
+            for h in range(2):
+                cols = slice(h * HALF, (h + 1) * HALF)
+                bank = psum.tile([P, PACK, HALF], F32, name="%s_bank%d" % (name, h))
+                for t in range(PACK):
+                    nc.tensor.matmul_mx(out=bank[:, t, :], lhsT=dealt_words[:, t * per:(t + 1) * per].bitcast(fmt),
+                                        lhsT_scale=dealt_plane[:, t * P:(t + 1) * P],
+                                        rhs=words[:, cols].bitcast(E5M2X4), rhs_scale=plane[:, cols], start=True, stop=True)
+                g = sbuf("%s_grouped%d" % (name, h), [P, HALF, PACK], BF16)
+                nc.scalar.copy(g[:], bank[:].rearrange("p t j -> p j t"))
+                grouped.append(g)
+            return grouped
+
+        deal(nc.scalar.copy, w_dealt[:].bitcast(U16), w_raw[:].bitcast(U16))
+        deal(nc.vector.tensor_copy, ws_dealt[:], ws_raw[:])
+        interleave(nc.scalar.copy, ka_grouped, ka_rows)
+        a_grouped = first_stage("a", l1, w_dealt, E2M1X4, ws_dealt)
+        deal(nc.scalar.copy, w2_dealt[:], w2_raw[:])
+        deal(nc.vector.tensor_copy, w2s_dealt[:], w2s_raw[:])
+        b_grouped = first_stage("b", l2, w2_dealt, E4M3X4, w2s_dealt)
+        kaq = quantize("ka", ka_grouped, U)
+        aq = [quantize("a%d" % h, a_grouped[h], HALF) for h in range(2)]
+
+        kb_bytes = [sbuf("kb_bytes%d" % x, [P, PACK, HALF], U8) for x in range(2)]
+        kb_grouped = [sbuf("kb_grouped%d" % x, [P, HALF, PACK], BF16) for x in range(2)]
+        kb_rows = sbuf("kb_rows", [P, PACK, HALF], BF16)
+
+        def look_up_b(x, t):
+            nc.vector.tensor_copy(kb_bytes[x][:, t, :], cb_t[t][:].indirect(l4[:, 8 * x:8 * x + 8]))
+
+        def second_stage(x, kbq, evacuate):
+            cols = slice(x * HALF, (x + 1) * HALF)
+            for h in range(2):
+                bank = psum.tile([P, HALF], F32, name="p_bank%d%d" % (x, h))
+                nc.tensor.matmul_mx(out=bank[:], lhsT=aq[h][0][:].bitcast(E4M3X4), lhsT_scale=aq[h][1][:],
+                                    rhs=kaq[0][:, cols].bitcast(E4M3X4), rhs_scale=kaq[1][:, cols], start=True, stop=False)
+                nc.tensor.matmul_mx(out=bank[:], lhsT=bq[h][0][:].bitcast(E4M3X4), lhsT_scale=bq[h][1][:],
+                                    rhs=kbq[0][:].bitcast(E4M3X4), rhs_scale=kbq[1][:], start=False, stop=True)
+                scores = sbuf("scores%d%d" % (x, h), [P, HALF], F32)
+                evacuate(scores[:], bank[:])
+                nc.scalar.activation(pages[h][:].indirect(l5[:, 8 * x:8 * x + 8]), scores[:], COPY, scale=sz_t[:, h:h + 1])
+
+        for t in range(PACK):
+            look_up_b(0, t)
+            nc.scalar.activation(kb_rows[:, t, :], kb_bytes[0][:, t, :].bitcast(FP8), COPY, scale=sb_t[:, t:t + 1])
+        bq = [quantize("b%d" % h, b_grouped[h], HALF) for h in range(2)]
+        look_up_b(1, 0)
+        interleave(nc.vector.tensor_copy, kb_grouped[0], kb_rows)
+        look_up_b(1, 1)
+        kbq0 = quantize("kb0", kb_grouped[0], HALF)
+        second_stage(0, kbq0, nc.scalar.copy)
+        look_up_b(1, 2)
+        look_up_b(1, 3)
+        for t in range(PACK):
+            nc.vector.tensor_scalar(kb_grouped[1][:, :, t], kb_bytes[1][:, t, :].bitcast(FP8), sb_t[:, t:t + 1], None, MULT)
+        kbq1 = quantize("kb1", kb_grouped[1], HALF)
+        second_stage(1, kbq1, nc.vector.tensor_copy)
+        for h in range(2):
+            nc.sync.dma_start(out[h * HALF:(h + 1) * HALF, :], pages[h][:])

@@ -30,25 +30,19 @@ def tile_list_scoredboth_kernel(tc, xt_words, xt_scales, w_words, w_scales, w2_w
         pool = ctx.enter_context(tc.tile_pool(name="pool", bufs=1))
         psum = ctx.enter_context(tc.psum_pool(name="psum", bufs=1))
 
-        def sbuf(name, shape, dtype):
-            return pool.tile(shape, dtype, name=name, align_bytes=64)
+        def sbuf(name, shape, dtype, tag=""):
+            return pool.tile(shape, dtype, name=name, tag=tag, align_bytes=64)
 
         def load_list(name, src):
             lst = sbuf(name, [P, 16], U16)
             nc.sync.dma_start(lst[:], src)
             return lst
 
-        def load_scale_rows(queue, plane, src, quads):
-            for q in quads:
-                queue.dma_start(plane[32 * q:32 * q + 4, :].bitcast(I32), src[0, 4 * q:4 * q + 4, :].bitcast(I32))
-
         xs = sbuf("xs", [P, T], U8)
-        ws_raw = sbuf("ws_raw", [P, R], U8)
-        w2s_raw = sbuf("w2s_raw", [P, R], U8)
+        ws = sbuf("ws", [P, R], U8)
         pages = [sbuf("page%d" % h, [P, E], F32) for h in range(2)]
         nc.vector.memset(xs[:].bitcast(I32), 0)
-        nc.vector.memset(ws_raw[:].bitcast(I32), 0)
-        nc.vector.memset(w2s_raw[:].bitcast(I32), 0)
+        nc.vector.memset(ws[:].bitcast(I32), 0)
         for h in range(2):
             nc.vector.memset(pages[h][:], 0.0)
 
@@ -59,36 +53,38 @@ def tile_list_scoredboth_kernel(tc, xt_words, xt_scales, w_words, w_scales, w2_w
         sa_t = sbuf("sa", [P, PACK], F32)
         sb_t = sbuf("sb", [P, PACK], F32)
         sz_t = sbuf("sz", [P, 2], F32)
-        xw = sbuf("xw", [P, T], U32)
-        w_raw = sbuf("w_raw", [P, 2 * R], U8)
-        w2_raw = sbuf("w2_raw", [P, R], U32)
+        xw = sbuf("xw", [P, T], U32, tag="xw")
+        ww = sbuf("ww", [P, 2 * R], U8)
+        w2w = sbuf("w2w", [P, R], U32)
+        ws_staged = sbuf("ws_staged", [4, 4, R // 4], I32, tag="ws_staged")
+        w2s_staged = sbuf("w2s_staged", [4, 4, R // 4], I32)
+
+        nc.gpsimd.dma_start(w2s_staged[:], w2_scales[0].bitcast(I32).rearrange("(q r) c -> r q c", r=4))
+        with nc.allow_non_contiguous_dma(reason="one weight a slot"):
+            nc.gpsimd.dma_start(sz_t[:], sz.rearrange("(h p) o -> p (h o)", h=2))
 
         l3 = load_list("l3", offs3)
         nc.sync.dma_start(ca_t[0][:], ca_rows[0])
-        nc.sync.dma_start(ca_t[1][:], ca_rows[1])
         nc.sync.dma_start(sa_t[:], sa.rearrange("(p t) o -> p (t o)", t=PACK))
-        nc.sync.dma_start(ca_t[2][:], ca_rows[2])
-        nc.sync.dma_start(ca_t[3][:], ca_rows[3])
+        for t in range(1, PACK):
+            nc.sync.dma_start(ca_t[t][:], ca_rows[t])
+        nc.sync.dma_start(ws_staged[:], w_scales[0].bitcast(I32).rearrange("(q r) c -> r q c", r=4))
         nc.sync.dma_start(xw[:].bitcast(I32), xt_words[0].rearrange("p c r -> p (c r)").bitcast(I32))
         l1 = load_list("l1", offs)
-        load_scale_rows(nc.sync, xs, xt_scales, range(4))
-        nc.sync.dma_start(w_raw[:].bitcast(I32), w_words[0].bitcast(I32))
+        for q in range(4):
+            nc.sync.dma_start(xs[32 * q:32 * q + 4, :].bitcast(I32), xt_scales[0, 4 * q:4 * q + 4, :].bitcast(I32))
+        nc.sync.dma_start(ww[:].bitcast(I32), w_words[0].bitcast(I32))
         l2 = load_list("l2", offs2)
-        nc.sync.dma_start(w2_raw[:].bitcast(I32), w2_words[0].rearrange("p c r -> p (c r)").bitcast(I32))
-        load_scale_rows(nc.sync, ws_raw, w_scales, range(4))
-        load_scale_rows(nc.sync, w2s_raw, w2_scales, range(4))
+        nc.sync.dma_start(w2w[:].bitcast(I32), w2_words[0].rearrange("p c r -> p (c r)").bitcast(I32))
         nc.sync.dma_start(cb_t[0][:], cb_rows[0])
         l4 = load_list("l4", offs4)
-        nc.sync.dma_start(cb_t[1][:], cb_rows[1])
-        nc.sync.dma_start(sb_t[:], sb.rearrange("(p t) o -> p (t o)", t=PACK))
-        for t in range(2, PACK):
+        for t in range(1, PACK):
             nc.sync.dma_start(cb_t[t][:], cb_rows[t])
+        nc.sync.dma_start(sb_t[:], sb.rearrange("(p t) o -> p (t o)", t=PACK))
         l5 = load_list("l5", offs5)
-        with nc.allow_non_contiguous_dma(reason="one weight a slot"):
-            nc.sync.dma_start(sz_t[:], sz.rearrange("(h p) o -> p (h o)", h=2))
 
-        def quantize(name, grouped, width):
-            codes = sbuf(name + "_codes", [P, width], U32)
+        def quantize(name, grouped, width, tag=""):
+            codes = sbuf(name + "_codes", [P, width], U32, tag=tag)
             plane = sbuf(name + "_plane", [P, width], U8)
             nc.vector.quantize_mx(out=codes[:].bitcast(E4M3X4), scales=plane[:], in_=grouped[:].rearrange("p u t -> p (u t)"))
             return codes, plane
@@ -102,77 +98,96 @@ def tile_list_scoredboth_kernel(tc, xt_words, xt_scales, w_words, w_scales, w2_w
         for t in range(PACK):
             nc.vector.tensor_copy(ka_bytes[:, t, :], ca_t[t][:].indirect(l3[:]))
             nc.scalar.activation(ka_rows[:, t, :], ka_bytes[:, t, :].bitcast(FP8), COPY, scale=sa_t[:, t:t + 1])
+        interleave(nc.scalar.copy, ka_grouped, ka_rows)
 
-        w_dealt = sbuf("w_dealt", [P, 2 * R], U8)
-        ws_dealt = sbuf("ws_dealt", [P, R], U8)
-        w2_dealt = sbuf("w2_dealt", [P, R], U32)
-        w2s_dealt = sbuf("w2s_dealt", [P, R], U8)
+        def spread(plane, staged):
+            for q in range(4):
+                nc.vector.tensor_copy(plane[32 * q:32 * q + 4, :].bitcast(I32), staged[:, q, :])
 
         def deal(copy, dst, src):
             copy(dst.rearrange("p (t m) -> p t m", t=PACK), src.rearrange("p (m t) -> p t m", t=PACK))
 
-        def first_stage(name, lst, dealt_words, fmt, dealt_plane):
+        w_dealt = sbuf("w_dealt", [P, 2 * R], U8, tag="dealt")
+        ws_dealt = sbuf("ws_dealt", [P, R], U8)
+        w2s_dealt = sbuf("w2s_dealt", [P, R], U8)
+        spread(ws, ws_staged)
+        w2s = sbuf("w2s", [P, R], U8, tag="ws_staged")
+        nc.vector.memset(w2s[:].bitcast(I32), 0)
+        spread(w2s, w2s_staged)
+        deal(nc.vector.tensor_copy, ws_dealt[:], ws[:])
+        deal(nc.vector.tensor_copy, w2s_dealt[:], w2s[:])
+        deal(nc.scalar.copy, w_dealt[:].bitcast(U16), ww[:].bitcast(U16))
+
+        def look_up_tokens(name, lst):
             words = sbuf(name + "_xw", [P, J], U32)
             plane = sbuf(name + "_xs", [P, J], U8)
             nc.vector.tensor_copy(words[:], xw[:].indirect(lst[:]))
             nc.vector.tensor_copy(plane[:], xs[:].indirect(lst[:]))
-            grouped = []
+            return words, plane
+
+        def project_only(name, h, tokens, dealt_words, fmt, dealt_plane):
+            cols = slice(h * HALF, (h + 1) * HALF)
             per = dealt_words.shape[1] // PACK
-            for h in range(2):
-                cols = slice(h * HALF, (h + 1) * HALF)
-                bank = psum.tile([P, PACK, HALF], F32, name="%s_bank%d" % (name, h))
-                for t in range(PACK):
-                    nc.tensor.matmul_mx(out=bank[:, t, :], lhsT=dealt_words[:, t * per:(t + 1) * per].bitcast(fmt),
-                                        lhsT_scale=dealt_plane[:, t * P:(t + 1) * P],
-                                        rhs=words[:, cols].bitcast(E5M2X4), rhs_scale=plane[:, cols], start=True, stop=True)
-                g = sbuf("%s_grouped%d" % (name, h), [P, HALF, PACK], BF16)
-                nc.scalar.copy(g[:], bank[:].rearrange("p t j -> p j t"))
-                grouped.append(g)
+            bank = psum.tile([P, PACK, HALF], F32, name="%s_bank%d" % (name, h))
+            for t in range(PACK):
+                nc.tensor.matmul_mx(out=bank[:, t, :], lhsT=dealt_words[:, t * per:(t + 1) * per].bitcast(fmt),
+                                    lhsT_scale=dealt_plane[:, t * P:(t + 1) * P],
+                                    rhs=tokens[0][:, cols].bitcast(E5M2X4), rhs_scale=tokens[1][:, cols], start=True, stop=True)
+            return bank
+
+        a_tokens = look_up_tokens("a", l1)
+        b_tokens = look_up_tokens("b", l2)
+        kaq = quantize("ka", ka_grouped, U, tag="xw")
+        a_grouped = sbuf("a_grouped", [P, J, PACK], BF16)
+        a_banks = [project_only("a", h, a_tokens, w_dealt, E2M1X4, ws_dealt) for h in range(2)]
+        nc.scalar.copy(a_grouped[:, 0:HALF, :], a_banks[0][:].rearrange("p t j -> p j t"))
+        w2_dealt = sbuf("w2_dealt", [P, R], U32, tag="dealt")
+        deal(nc.scalar.copy, w2_dealt[:], w2w[:])
+        nc.scalar.copy(a_grouped[:, HALF:J, :], a_banks[1][:].rearrange("p t j -> p j t"))
+
+        def keys_of_second_store(x, looked_up):
+            grouped = sbuf("kb_grouped%d" % x, [P, HALF, PACK], BF16)
+            for t in range(PACK):
+                nc.vector.tensor_copy(looked_up[t], cb_t[t][:].indirect(l4[:, 8 * x:8 * x + 8]))
+            for t in range(PACK):
+                nc.vector.tensor_scalar(grouped[:, :, t], looked_up[t].bitcast(FP8), sb_t[:, t:t + 1], None, MULT)
             return grouped
 
-        deal(nc.scalar.copy, w_dealt[:].bitcast(U16), w_raw[:].bitcast(U16))
-        deal(nc.vector.tensor_copy, ws_dealt[:], ws_raw[:])
-        interleave(nc.scalar.copy, ka_grouped, ka_rows)
-        a_grouped = first_stage("a", l1, w_dealt, E2M1X4, ws_dealt)
-        deal(nc.scalar.copy, w2_dealt[:], w2_raw[:])
-        deal(nc.vector.tensor_copy, w2s_dealt[:], w2s_raw[:])
-        b_grouped = first_stage("b", l2, w2_dealt, E4M3X4, w2s_dealt)
-        kaq = quantize("ka", ka_grouped, U)
-        aq = [quantize("a%d" % h, a_grouped[h], HALF) for h in range(2)]
+        kb_grouped0 = keys_of_second_store(0, [sbuf("kb_first%d" % t, [P, HALF], U8, tag="kb_first%d" % t)[:] for t in range(PACK)])
+        b_grouped = [sbuf("b_grouped%d" % h, [P, HALF, PACK], BF16, tag="b_grouped%d" % h) for h in range(2)]
+        for h in range(2):
+            bank = project_only("b", h, b_tokens, w2_dealt, E4M3X4, w2s_dealt)
+            nc.scalar.copy(b_grouped[h][:], bank[:].rearrange("p t j -> p j t"))
+        a_codes, a_plane = quantize("a", a_grouped, J, tag="kb_first0")
+        aq = [(a_codes[:, h * HALF:(h + 1) * HALF], a_plane[:, h * HALF:(h + 1) * HALF]) for h in range(2)]
+        kbq0 = quantize("kb0", kb_grouped0, HALF)
+        bq = [quantize("b%d" % h, b_grouped[h], HALF, tag="kb_first%d" % (h + 1)) for h in range(2)]
 
-        kb_bytes = [sbuf("kb_bytes%d" % x, [P, PACK, HALF], U8) for x in range(2)]
-        kb_grouped = [sbuf("kb_grouped%d" % x, [P, HALF, PACK], BF16) for x in range(2)]
-        kb_rows = sbuf("kb_rows", [P, PACK, HALF], BF16)
-
-        def look_up_b(x, t):
-            nc.vector.tensor_copy(kb_bytes[x][:, t, :], cb_t[t][:].indirect(l4[:, 8 * x:8 * x + 8]))
-
-        def second_stage(x, kbq, evacuate):
+        def score(x, h, kbq, dst):
             cols = slice(x * HALF, (x + 1) * HALF)
-            for h in range(2):
-                bank = psum.tile([P, HALF], F32, name="p_bank%d%d" % (x, h))
-                nc.tensor.matmul_mx(out=bank[:], lhsT=aq[h][0][:].bitcast(E4M3X4), lhsT_scale=aq[h][1][:],
-                                    rhs=kaq[0][:, cols].bitcast(E4M3X4), rhs_scale=kaq[1][:, cols], start=True, stop=False)
-                nc.tensor.matmul_mx(out=bank[:], lhsT=bq[h][0][:].bitcast(E4M3X4), lhsT_scale=bq[h][1][:],
-                                    rhs=kbq[0][:].bitcast(E4M3X4), rhs_scale=kbq[1][:], start=False, stop=True)
-                scores = sbuf("scores%d%d" % (x, h), [P, HALF], F32)
-                evacuate(scores[:], bank[:])
-                nc.scalar.activation(pages[h][:].indirect(l5[:, 8 * x:8 * x + 8]), scores[:], COPY, scale=sz_t[:, h:h + 1])
+            nc.tensor.matmul_mx(out=dst, lhsT=aq[h][0].bitcast(E4M3X4), lhsT_scale=aq[h][1],
+                                rhs=kaq[0][:, cols].bitcast(E4M3X4), rhs_scale=kaq[1][:, cols], start=True, stop=False)
+            nc.tensor.matmul_mx(out=dst, lhsT=bq[h][0][:].bitcast(E4M3X4), lhsT_scale=bq[h][1][:],
+                                rhs=kbq[0][:].bitcast(E4M3X4), rhs_scale=kbq[1][:], start=False, stop=True)
 
-        for t in range(PACK):
-            look_up_b(0, t)
-            nc.scalar.activation(kb_rows[:, t, :], kb_bytes[0][:, t, :].bitcast(FP8), COPY, scale=sb_t[:, t:t + 1])
-        bq = [quantize("b%d" % h, b_grouped[h], HALF) for h in range(2)]
-        look_up_b(1, 0)
-        interleave(nc.vector.tensor_copy, kb_grouped[0], kb_rows)
-        look_up_b(1, 1)
-        kbq0 = quantize("kb0", kb_grouped[0], HALF)
-        second_stage(0, kbq0, nc.scalar.copy)
-        look_up_b(1, 2)
-        look_up_b(1, 3)
-        for t in range(PACK):
-            nc.vector.tensor_scalar(kb_grouped[1][:, :, t], kb_bytes[1][:, t, :].bitcast(FP8), sb_t[:, t:t + 1], None, MULT)
-        kbq1 = quantize("kb1", kb_grouped[1], HALF)
-        second_stage(1, kbq1, nc.vector.tensor_copy)
+        def put(x, h, scores):
+            nc.scalar.activation(pages[h][:].indirect(l5[:, 8 * x:8 * x + 8]), scores, COPY, scale=sz_t[:, h:h + 1])
+
+        first_bank = psum.tile([P, 2, HALF], F32, name="first_bank")
+        first_scores = sbuf("first_scores", [P, 2, HALF], F32)
+        for h in range(2):
+            score(0, h, kbq0, first_bank[:, h, :])
+        nc.scalar.copy(first_scores[:], first_bank[:])
+        for h in range(2):
+            put(0, h, first_scores[:, h, :])
+
+        kb_second = sbuf("kb_second", [P, PACK, HALF], U8, tag="b_grouped0")
+        kbq1 = quantize("kb1", keys_of_second_store(1, [kb_second[:, t, :] for t in range(PACK)]), HALF)
+        for h in range(2):
+            bank = psum.tile([P, HALF], F32, name="second_bank%d" % h)
+            score(1, h, kbq1, bank[:])
+            scores = sbuf("second_scores%d" % h, [P, HALF], F32)
+            nc.vector.tensor_copy(scores[:], bank[:])
+            put(1, h, scores[:])
         for h in range(2):
             nc.sync.dma_start(out[h * HALF:(h + 1) * HALF, :], pages[h][:])

@@ -60,8 +60,6 @@ def tile_list_scoredboth_kernel(tc, xt_words, xt_scales, w_words, w_scales, w2_w
         w2s_staged = sbuf("w2s_staged", [4, 4, R // 4], I32)
 
         nc.gpsimd.dma_start(w2s_staged[:], w2_scales[0].bitcast(I32).rearrange("(q r) c -> r q c", r=4))
-        with nc.allow_non_contiguous_dma(reason="one weight a slot"):
-            nc.gpsimd.dma_start(sz_t[:], sz.rearrange("(h p) o -> p (h o)", h=2))
 
         l3 = load_list("l3", offs3)
         nc.sync.dma_start(ca_t[0][:], ca_rows[0])
@@ -71,10 +69,10 @@ def tile_list_scoredboth_kernel(tc, xt_words, xt_scales, w_words, w_scales, w2_w
         nc.sync.dma_start(ws_staged[:], w_scales[0].bitcast(I32).rearrange("(q r) c -> r q c", r=4))
         nc.sync.dma_start(xw[:].bitcast(I32), xt_words[0].rearrange("p c r -> p (c r)").bitcast(I32))
         l1 = load_list("l1", offs)
+        l2 = load_list("l2", offs2)
+        nc.sync.dma_start(ww[:].bitcast(I32), w_words[0].bitcast(I32))
         for q in range(4):
             nc.sync.dma_start(xs[32 * q:32 * q + 4, :].bitcast(I32), xt_scales[0, 4 * q:4 * q + 4, :].bitcast(I32))
-        nc.sync.dma_start(ww[:].bitcast(I32), w_words[0].bitcast(I32))
-        l2 = load_list("l2", offs2)
         nc.sync.dma_start(w2w[:].bitcast(I32), w2_words[0].rearrange("p c r -> p (c r)").bitcast(I32))
         nc.sync.dma_start(cb_t[0][:], cb_rows[0])
         l4 = load_list("l4", offs4)
@@ -82,6 +80,8 @@ def tile_list_scoredboth_kernel(tc, xt_words, xt_scales, w_words, w_scales, w2_w
             nc.sync.dma_start(cb_t[t][:], cb_rows[t])
         nc.sync.dma_start(sb_t[:], sb.rearrange("(p t) o -> p (t o)", t=PACK))
         l5 = load_list("l5", offs5)
+        with nc.allow_non_contiguous_dma(reason="one weight a slot"):
+            nc.sync.dma_start(sz_t[:], sz.rearrange("(h p) o -> p (h o)", h=2))
 
         def quantize(name, grouped, width, tag=""):
             codes = sbuf(name + "_codes", [P, width], U32, tag=tag)
@@ -107,7 +107,8 @@ def tile_list_scoredboth_kernel(tc, xt_words, xt_scales, w_words, w_scales, w2_w
         def deal(copy, dst, src):
             copy(dst.rearrange("p (t m) -> p t m", t=PACK), src.rearrange("p (m t) -> p t m", t=PACK))
 
-        w_dealt = sbuf("w_dealt", [P, 2 * R], U8, tag="dealt")
+        w_dealt = sbuf("w_dealt", [P, 2 * R], U8)
+        w2_dealt = sbuf("w2_dealt", [P, R], U32)
         ws_dealt = sbuf("ws_dealt", [P, R], U8)
         w2s_dealt = sbuf("w2s_dealt", [P, R], U8)
         spread(ws, ws_staged)
@@ -117,13 +118,15 @@ def tile_list_scoredboth_kernel(tc, xt_words, xt_scales, w_words, w_scales, w2_w
         deal(nc.vector.tensor_copy, ws_dealt[:], ws[:])
         deal(nc.vector.tensor_copy, w2s_dealt[:], w2s[:])
         deal(nc.scalar.copy, w_dealt[:].bitcast(U16), ww[:].bitcast(U16))
+        deal(nc.scalar.copy, w2_dealt[:], w2w[:])
 
-        def look_up_tokens(name, lst):
-            words = sbuf(name + "_xw", [P, J], U32)
-            plane = sbuf(name + "_xs", [P, J], U8)
-            nc.vector.tensor_copy(words[:], xw[:].indirect(lst[:]))
-            nc.vector.tensor_copy(plane[:], xs[:].indirect(lst[:]))
-            return words, plane
+        token_words = [sbuf("token_words%d" % n, [P, J], U32) for n in range(2)]
+        token_planes = [sbuf("token_plane%d" % n, [P, J], U8) for n in range(2)]
+        for n, lst in enumerate((l1, l2)):
+            nc.vector.tensor_copy(token_words[n][:], xw[:].indirect(lst[:]))
+        for n, lst in enumerate((l1, l2)):
+            nc.vector.tensor_copy(token_planes[n][:], xs[:].indirect(lst[:]))
+        a_tokens, b_tokens = zip(token_words, token_planes)
 
         def project_only(name, h, tokens, dealt_words, fmt, dealt_plane):
             cols = slice(h * HALF, (h + 1) * HALF)
@@ -135,33 +138,32 @@ def tile_list_scoredboth_kernel(tc, xt_words, xt_scales, w_words, w_scales, w2_w
                                     rhs=tokens[0][:, cols].bitcast(E5M2X4), rhs_scale=tokens[1][:, cols], start=True, stop=True)
             return bank
 
-        a_tokens = look_up_tokens("a", l1)
-        b_tokens = look_up_tokens("b", l2)
         kaq = quantize("ka", ka_grouped, U, tag="xw")
         a_grouped = sbuf("a_grouped", [P, J, PACK], BF16)
         a_banks = [project_only("a", h, a_tokens, w_dealt, E2M1X4, ws_dealt) for h in range(2)]
         nc.scalar.copy(a_grouped[:, 0:HALF, :], a_banks[0][:].rearrange("p t j -> p j t"))
-        w2_dealt = sbuf("w2_dealt", [P, R], U32, tag="dealt")
-        deal(nc.scalar.copy, w2_dealt[:], w2w[:])
         nc.scalar.copy(a_grouped[:, HALF:J, :], a_banks[1][:].rearrange("p t j -> p j t"))
 
         def keys_of_second_store(x, looked_up):
-            grouped = sbuf("kb_grouped%d" % x, [P, HALF, PACK], BF16)
+            rows = sbuf("kb_rows%d" % x, [P, PACK, HALF], BF16)
             for t in range(PACK):
                 nc.vector.tensor_copy(looked_up[t], cb_t[t][:].indirect(l4[:, 8 * x:8 * x + 8]))
             for t in range(PACK):
-                nc.vector.tensor_scalar(grouped[:, :, t], looked_up[t].bitcast(FP8), sb_t[:, t:t + 1], None, MULT)
-            return grouped
+                nc.vector.tensor_scalar(rows[:, t, :], looked_up[t].bitcast(FP8), sb_t[:, t:t + 1], None, MULT)
+            return rows
 
-        kb_grouped0 = keys_of_second_store(0, [sbuf("kb_first%d" % t, [P, HALF], U8, tag="kb_first%d" % t)[:] for t in range(PACK)])
+        kb_grouped = [sbuf("kb_grouped%d" % x, [P, HALF, PACK], BF16) for x in range(2)]
+        kb_rows0 = keys_of_second_store(0, [sbuf("kb_first%d" % t, [P, HALF], U8, tag="kb_first%d" % t)[:] for t in range(PACK)])
         b_grouped = [sbuf("b_grouped%d" % h, [P, HALF, PACK], BF16, tag="b_grouped%d" % h) for h in range(2)]
         for h in range(2):
             bank = project_only("b", h, b_tokens, w2_dealt, E4M3X4, w2s_dealt)
             nc.scalar.copy(b_grouped[h][:], bank[:].rearrange("p t j -> p j t"))
         a_codes, a_plane = quantize("a", a_grouped, J, tag="kb_first0")
         aq = [(a_codes[:, h * HALF:(h + 1) * HALF], a_plane[:, h * HALF:(h + 1) * HALF]) for h in range(2)]
-        kbq0 = quantize("kb0", kb_grouped0, HALF)
-        bq = [quantize("b%d" % h, b_grouped[h], HALF, tag="kb_first%d" % (h + 1)) for h in range(2)]
+        interleave(nc.vector.tensor_copy, kb_grouped[0], kb_rows0)
+        bq = [quantize("b0", b_grouped[0], HALF, tag="kb_first1")]
+        kbq0 = quantize("kb0", kb_grouped[0], HALF)
+        bq.append(quantize("b1", b_grouped[1], HALF, tag="kb_first2"))
 
         def score(x, h, kbq, dst):
             cols = slice(x * HALF, (x + 1) * HALF)
@@ -182,7 +184,8 @@ def tile_list_scoredboth_kernel(tc, xt_words, xt_scales, w_words, w_scales, w2_w
             put(0, h, first_scores[:, h, :])
 
         kb_second = sbuf("kb_second", [P, PACK, HALF], U8, tag="b_grouped0")
-        kbq1 = quantize("kb1", keys_of_second_store(1, [kb_second[:, t, :] for t in range(PACK)]), HALF)
+        interleave(nc.vector.tensor_copy, kb_grouped[1], keys_of_second_store(1, [kb_second[:, t, :] for t in range(PACK)]))
+        kbq1 = quantize("kb1", kb_grouped[1], HALF)
         for h in range(2):
             bank = psum.tile([P, HALF], F32, name="second_bank%d" % h)
             score(1, h, kbq1, bank[:])

@@ -38,9 +38,11 @@ def tile_list_scoredboth_kernel(tc, xt_words, xt_scales, w_words, w_scales, w2_w
             nc.sync.dma_start(lst[:], src)
             return lst
 
-        xs = sbuf("xs", [P, T], U8)
+        xs = sbuf("xs", [P, T], U8, tag="xs")
         ws = sbuf("ws", [P, R], U8)
+        w2s = sbuf("w2s", [P, R], U8)
         pages = [sbuf("page%d" % h, [P, E], F32) for h in range(2)]
+        nc.vector.memset(w2s[:].bitcast(I32), 0)
         nc.vector.memset(xs[:].bitcast(I32), 0)
         nc.vector.memset(ws[:].bitcast(I32), 0)
         for h in range(2):
@@ -53,13 +55,13 @@ def tile_list_scoredboth_kernel(tc, xt_words, xt_scales, w_words, w_scales, w2_w
         sa_t = sbuf("sa", [P, PACK], F32)
         sb_t = sbuf("sb", [P, PACK], F32)
         sz_t = sbuf("sz", [P, 2], F32)
-        xw = sbuf("xw", [P, T], U32, tag="xw")
+        xw = sbuf("xw", [P, T], U32)
         ww = sbuf("ww", [P, 2 * R], U8)
         w2w = sbuf("w2w", [P, R], U32)
-        ws_staged = sbuf("ws_staged", [4, 4, R // 4], I32, tag="ws_staged")
-        w2s_staged = sbuf("w2s_staged", [4, 4, R // 4], I32)
+        ws_staged = sbuf("ws_staged", [4, 4, R // 4], I32)
 
-        nc.gpsimd.dma_start(w2s_staged[:], w2_scales[0].bitcast(I32).rearrange("(q r) c -> r q c", r=4))
+        for q in range(4):
+            nc.gpsimd.dma_start(w2s[32 * q:32 * q + 4, :].bitcast(I32), w2_scales[0, 4 * q:4 * q + 4, :].bitcast(I32))
 
         l3 = load_list("l3", offs3)
         nc.sync.dma_start(ca_t[0][:], ca_rows[0])
@@ -70,9 +72,9 @@ def tile_list_scoredboth_kernel(tc, xt_words, xt_scales, w_words, w_scales, w2_w
         nc.sync.dma_start(xw[:].bitcast(I32), xt_words[0].rearrange("p c r -> p (c r)").bitcast(I32))
         l1 = load_list("l1", offs)
         l2 = load_list("l2", offs2)
-        nc.sync.dma_start(ww[:].bitcast(I32), w_words[0].bitcast(I32))
         for q in range(4):
             nc.sync.dma_start(xs[32 * q:32 * q + 4, :].bitcast(I32), xt_scales[0, 4 * q:4 * q + 4, :].bitcast(I32))
+        nc.sync.dma_start(ww[:].bitcast(I32), w_words[0].bitcast(I32))
         nc.sync.dma_start(w2w[:].bitcast(I32), w2_words[0].rearrange("p c r -> p (c r)").bitcast(I32))
         nc.sync.dma_start(cb_t[0][:], cb_rows[0])
         l4 = load_list("l4", offs4)
@@ -94,7 +96,7 @@ def tile_list_scoredboth_kernel(tc, xt_words, xt_scales, w_words, w_scales, w2_w
 
         ka_bytes = sbuf("ka_bytes", [P, PACK, U], U8)
         ka_rows = sbuf("ka_rows", [P, PACK, U], BF16)
-        ka_grouped = sbuf("ka_grouped", [P, U, PACK], BF16)
+        ka_grouped = sbuf("ka_grouped", [P, U, PACK], BF16, tag="ka_grouped")
         for t in range(PACK):
             nc.vector.tensor_copy(ka_bytes[:, t, :], ca_t[t][:].indirect(l3[:]))
             nc.scalar.activation(ka_rows[:, t, :], ka_bytes[:, t, :].bitcast(FP8), COPY, scale=sa_t[:, t:t + 1])
@@ -110,13 +112,8 @@ def tile_list_scoredboth_kernel(tc, xt_words, xt_scales, w_words, w_scales, w2_w
         w_dealt = sbuf("w_dealt", [P, 2 * R], U8)
         w2_dealt = sbuf("w2_dealt", [P, R], U32)
         ws_dealt = sbuf("ws_dealt", [P, R], U8)
-        w2s_dealt = sbuf("w2s_dealt", [P, R], U8)
         spread(ws, ws_staged)
-        w2s = sbuf("w2s", [P, R], U8, tag="ws_staged")
-        nc.vector.memset(w2s[:].bitcast(I32), 0)
-        spread(w2s, w2s_staged)
         deal(nc.vector.tensor_copy, ws_dealt[:], ws[:])
-        deal(nc.vector.tensor_copy, w2s_dealt[:], w2s[:])
         deal(nc.scalar.copy, w_dealt[:].bitcast(U16), ww[:].bitcast(U16))
         deal(nc.scalar.copy, w2_dealt[:], w2w[:])
 
@@ -138,7 +135,9 @@ def tile_list_scoredboth_kernel(tc, xt_words, xt_scales, w_words, w_scales, w2_w
                                     rhs=tokens[0][:, cols].bitcast(E5M2X4), rhs_scale=tokens[1][:, cols], start=True, stop=True)
             return bank
 
-        kaq = quantize("ka", ka_grouped, U, tag="xw")
+        kaq = quantize("ka", ka_grouped, U, tag="xs")
+        w2s_dealt = sbuf("w2s_dealt", [P, R], U8, tag="ka_grouped")
+        deal(nc.vector.tensor_copy, w2s_dealt[:], w2s[:])
         a_grouped = sbuf("a_grouped", [P, J, PACK], BF16)
         a_banks = [project_only("a", h, a_tokens, w_dealt, E2M1X4, ws_dealt) for h in range(2)]
         nc.scalar.copy(a_grouped[:, 0:HALF, :], a_banks[0][:].rearrange("p t j -> p j t"))

from contextlib import ExitStack

import concourse.mybir as mybir

K, T, J, R, V, U, E = 512, 2048, 256, 512, 1024, 256, 512
FLOPS = 2 * (2 * K * R * J) + 2 * (2 * R * J * U)

F32 = mybir.dt.float32
BF16 = mybir.dt.bfloat16
I32 = mybir.dt.int32
U32 = mybir.dt.uint32
U16 = mybir.dt.uint16
U8 = mybir.dt.uint8
FP8 = mybir.dt.float8_e4m3fn
E4M3X4 = mybir.dt.float8_e4m3fn_x4
E5M2X4 = mybir.dt.float8_e5m2_x4
E2M1X4 = mybir.dt.float4_e2m1fn_x4
COPY = mybir.ActivationFunctionType.Copy
MULT = mybir.AluOpType.mult

P = 128
PACK = 4
HALF = 128


def tile_list_scoredboth_kernel(tc, xt_words, xt_scales, w_words, w_scales, w2_words, w2_scales, ca, cb, sa, sb, sz,
                                   offs, offs2, offs3, offs4, offs5, out):
    nc = tc.nc
    with ExitStack() as ctx:
        pool = ctx.enter_context(tc.tile_pool(name="pool", bufs=1))
        psum = ctx.enter_context(tc.psum_pool(name="psum", bufs=1))

        def sbuf(name, shape, dtype, tag=""):
            return pool.tile(shape, dtype, name=name, tag=tag, align_bytes=64)

        def load_list(name, src):
            lst = sbuf(name, [P, 16], U16)
            nc.sync.dma_start(lst[:], src)
            return lst

        xs = sbuf("xs", [P, T], U8, tag="xs")
        ws = sbuf("ws", [P, R], U8)
        w2s = sbuf("w2s", [P, R], U8)
        pages = [sbuf("page%d" % h, [P, E], F32) for h in range(2)]
        nc.vector.memset(w2s[:].bitcast(I32), 0)
        nc.vector.memset(xs[:].bitcast(I32), 0)
        nc.vector.memset(ws[:].bitcast(I32), 0)
        for h in range(2):
            nc.vector.memset(pages[h][:], 0.0)

        ca_rows = ca.rearrange("(p t) v -> t p v", t=PACK)
        cb_rows = cb.rearrange("(p t) v -> t p v", t=PACK)
        ca_t = [sbuf("ca%d" % t, [P, V], U8) for t in range(PACK)]
        cb_t = [sbuf("cb%d" % t, [P, V], U8) for t in range(PACK)]
        sa_t = sbuf("sa", [P, PACK], F32)
        sb_t = sbuf("sb", [P, PACK], F32)
        sz_t = sbuf("sz", [P, 2], F32)
        xw = sbuf("xw", [P, T], U32)
        ww = sbuf("ww", [P, 2 * R], U8)
        w2w = sbuf("w2w", [P, R], U32)
        ws_staged = sbuf("ws_staged", [4, 4, R // 4], I32)

        for q in range(4):
            nc.gpsimd.dma_start(w2s[32 * q:32 * q + 4, :].bitcast(I32), w2_scales[0, 4 * q:4 * q + 4, :].bitcast(I32))

        l3 = load_list("l3", offs3)
        nc.sync.dma_start(ca_t[0][:], ca_rows[0])
        nc.sync.dma_start(sa_t[:], sa.rearrange("(p t) o -> p (t o)", t=PACK))
        for t in range(1, PACK):
            nc.sync.dma_start(ca_t[t][:], ca_rows[t])
        nc.sync.dma_start(ws_staged[:], w_scales[0].bitcast(I32).rearrange("(q r) c -> r q c", r=4))
        nc.sync.dma_start(xw[:].bitcast(I32), xt_words[0].rearrange("p c r -> p (c r)").bitcast(I32))
        l1 = load_list("l1", offs)
        l2 = load_list("l2", offs2)
        for q in range(4):
            nc.sync.dma_start(xs[32 * q:32 * q + 4, :].bitcast(I32), xt_scales[0, 4 * q:4 * q + 4, :].bitcast(I32))
        nc.sync.dma_start(ww[:].bitcast(I32), w_words[0].bitcast(I32))
        nc.sync.dma_start(w2w[:].bitcast(I32), w2_words[0].rearrange("p c r -> p (c r)").bitcast(I32))
        nc.sync.dma_start(cb_t[0][:], cb_rows[0])
        l4 = load_list("l4", offs4)
        for t in range(1, PACK):
            nc.sync.dma_start(cb_t[t][:], cb_rows[t])
        nc.sync.dma_start(sb_t[:], sb.rearrange("(p t) o -> p (t o)", t=PACK))
        l5 = load_list("l5", offs5)
        with nc.allow_non_contiguous_dma(reason="one weight a slot"):
            nc.sync.dma_start(sz_t[:], sz.rearrange("(h p) o -> p (h o)", h=2))

        def quantize(name, grouped, width, tag=""):
            codes = sbuf(name + "_codes", [P, width], U32, tag=tag)
            plane = sbuf(name + "_plane", [P, width], U8)
            nc.vector.quantize_mx(out=codes[:].bitcast(E4M3X4), scales=plane[:], in_=grouped[:].rearrange("p u t -> p (u t)"))
            return codes, plane

        def interleave(copy, grouped, rows):
            copy(grouped[:].rearrange("p (c i) t -> p c t i", i=4), rows[:].rearrange("p t (c i) -> p c t i", i=4))

        ka_bytes = sbuf("ka_bytes", [P, PACK, U], U8)
        ka_rows = sbuf("ka_rows", [P, PACK, U], BF16)
        ka_grouped = sbuf("ka_grouped", [P, U, PACK], BF16, tag="ka_grouped")
        for t in range(PACK):
            nc.vector.tensor_copy(ka_bytes[:, t, :], ca_t[t][:].indirect(l3[:]))
            nc.scalar.activation(ka_rows[:, t, :], ka_bytes[:, t, :].bitcast(FP8), COPY, scale=sa_t[:, t:t + 1])
        interleave(nc.scalar.copy, ka_grouped, ka_rows)

        def spread(plane, staged):
            for q in range(4):
                nc.vector.tensor_copy(plane[32 * q:32 * q + 4, :].bitcast(I32), staged[:, q, :])

        def deal(copy, dst, src):
            copy(dst.rearrange("p (t m) -> p t m", t=PACK), src.rearrange("p (m t) -> p t m", t=PACK))

        w_dealt = sbuf("w_dealt", [P, 2 * R], U8)
        w2_dealt = sbuf("w2_dealt", [P, R], U32)
        ws_dealt = sbuf("ws_dealt", [P, R], U8)
        spread(ws, ws_staged)
        deal(nc.vector.tensor_copy, ws_dealt[:], ws[:])
        deal(nc.scalar.copy, w_dealt[:].bitcast(U16), ww[:].bitcast(U16))
        deal(nc.scalar.copy, w2_dealt[:], w2w[:])

        token_words = [sbuf("token_words%d" % n, [P, J], U32) for n in range(2)]
        token_planes = [sbuf("token_plane%d" % n, [P, J], U8) for n in range(2)]
        for n, lst in enumerate((l1, l2)):
            nc.vector.tensor_copy(token_words[n][:], xw[:].indirect(lst[:]))
        for n, lst in enumerate((l1, l2)):
            nc.vector.tensor_copy(token_planes[n][:], xs[:].indirect(lst[:]))
        a_tokens, b_tokens = zip(token_words, token_planes)

        def project_only(name, h, tokens, dealt_words, fmt, dealt_plane):
            cols = slice(h * HALF, (h + 1) * HALF)
            per = dealt_words.shape[1] // PACK
            bank = psum.tile([P, PACK, HALF], F32, name="%s_bank%d" % (name, h))
            for t in range(PACK):
                nc.tensor.matmul_mx(out=bank[:, t, :], lhsT=dealt_words[:, t * per:(t + 1) * per].bitcast(fmt),
                                    lhsT_scale=dealt_plane[:, t * P:(t + 1) * P],
                                    rhs=tokens[0][:, cols].bitcast(E5M2X4), rhs_scale=tokens[1][:, cols], start=True, stop=True)
            return bank

        kaq = quantize("ka", ka_grouped, U, tag="xs")
        w2s_dealt = sbuf("w2s_dealt", [P, R], U8, tag="ka_grouped")
        deal(nc.vector.tensor_copy, w2s_dealt[:], w2s[:])
        a_grouped = sbuf("a_grouped", [P, J, PACK], BF16)
        a_banks = [project_only("a", h, a_tokens, w_dealt, E2M1X4, ws_dealt) for h in range(2)]
        nc.scalar.copy(a_grouped[:, 0:HALF, :], a_banks[0][:].rearrange("p t j -> p j t"))
        nc.scalar.copy(a_grouped[:, HALF:J, :], a_banks[1][:].rearrange("p t j -> p j t"))

        def keys_of_second_store(x, looked_up):
            rows = sbuf("kb_rows%d" % x, [P, PACK, HALF], BF16)
            for t in range(PACK):
                nc.vector.tensor_copy(looked_up[t], cb_t[t][:].indirect(l4[:, 8 * x:8 * x + 8]))
            for t in range(PACK):
                nc.vector.tensor_scalar(rows[:, t, :], looked_up[t].bitcast(FP8), sb_t[:, t:t + 1], None, MULT)
            return rows

        kb_grouped = [sbuf("kb_grouped%d" % x, [P, HALF, PACK], BF16) for x in range(2)]
        kb_rows0 = keys_of_second_store(0, [sbuf("kb_first%d" % t, [P, HALF], U8, tag="kb_first%d" % t)[:] for t in range(PACK)])
        b_grouped = [sbuf("b_grouped%d" % h, [P, HALF, PACK], BF16, tag="b_grouped%d" % h) for h in range(2)]
        for h in range(2):
            bank = project_only("b", h, b_tokens, w2_dealt, E4M3X4, w2s_dealt)
            nc.scalar.copy(b_grouped[h][:], bank[:].rearrange("p t j -> p j t"))
        a_codes, a_plane = quantize("a", a_grouped, J, tag="kb_first0")
        aq = [(a_codes[:, h * HALF:(h + 1) * HALF], a_plane[:, h * HALF:(h + 1) * HALF]) for h in range(2)]
        interleave(nc.vector.tensor_copy, kb_grouped[0], kb_rows0)
        bq = [quantize("b0", b_grouped[0], HALF, tag="kb_first1")]
        kbq0 = quantize("kb0", kb_grouped[0], HALF)
        bq.append(quantize("b1", b_grouped[1], HALF, tag="kb_first2"))

        def score(x, h, kbq, dst):
            cols = slice(x * HALF, (x + 1) * HALF)
            nc.tensor.matmul_mx(out=dst, lhsT=aq[h][0].bitcast(E4M3X4), lhsT_scale=aq[h][1],
                                rhs=kaq[0][:, cols].bitcast(E4M3X4), rhs_scale=kaq[1][:, cols], start=True, stop=False)
            nc.tensor.matmul_mx(out=dst, lhsT=bq[h][0][:].bitcast(E4M3X4), lhsT_scale=bq[h][1][:],
                                rhs=kbq[0][:].bitcast(E4M3X4), rhs_scale=kbq[1][:], start=False, stop=True)

        def put(x, h, scores):
            nc.scalar.activation(pages[h][:].indirect(l5[:, 8 * x:8 * x + 8]), scores, COPY, scale=sz_t[:, h:h + 1])

        first_bank = psum.tile([P, 2, HALF], F32, name="first_bank")
        first_scores = sbuf("first_scores", [P, 2, HALF], F32)
        for h in range(2):
            score(0, h, kbq0, first_bank[:, h, :])
        nc.scalar.copy(first_scores[:], first_bank[:])
        for h in range(2):
            put(0, h, first_scores[:, h, :])

        kb_second = sbuf("kb_second", [P, PACK, HALF], U8, tag="b_grouped0")
        interleave(nc.vector.tensor_copy, kb_grouped[1], keys_of_second_store(1, [kb_second[:, t, :] for t in range(PACK)]))
        kbq1 = quantize("kb1", kb_grouped[1], HALF)
        for h in range(2):
            bank = psum.tile([P, HALF], F32, name="second_bank%d" % h)
            score(1, h, kbq1, bank[:])
            scores = sbuf("second_scores%d" % h, [P, HALF], F32)
            nc.vector.tensor_copy(scores[:], bank[:])
            put(1, h, scores[:])
        for h in range(2):
            nc.sync.dma_start(out[h * HALF:(h + 1) * HALF, :], pages[h][:])
